import numpy as np
CORES = [43,171,299,427]
N = 4
ROOT = 2
def setup_inputs(rng):
    return {"x": rng.standard_normal((N, 128, 128), dtype=np.float32)}
def reference(x):
    y = np.full((N, 128, N * 128), np.nan, x.dtype)
    y[ROOT] = np.concatenate(list(x), axis=1)
    return {"y": y}

W = 128
ENGINES = 8

SCRATCH = {
    "buf": ("sbuf", [128, 3 * W], "float32"),
}
SEMAPHORES = [
    "loaded",
    "sent",
    "arr0",
    "arr1",
    "arr3",
    "stored_hw",
    "stored_g",
]


def rank_program(g, core, T, topo):
    cores = T.cores
    root_rank = 2 if T.root is None else T.root
    root = cores[root_rank]
    helper = (cores[1] // 8) * 8 + 1
    slot = {0: T.buf[:, 0:W], 1: T.buf[:, W:2 * W], 3: T.buf[:, 2 * W:3 * W]}
    arr = {0: T.sem.arr0, 1: T.sem.arr1, 3: T.sem.arr3}

    def send(dst, out_ap, remote_sem):
        rid, pid = topo.addr(dst, core)
        g.remote_dma(out_ap, slot[0], remote_sem, T.sem.sent, pid, rid, topo.mask(core, dst))
        g.wait_ge(T.sem.sent, ENGINES)

    if core == helper:
        g.wait_ge(T.sem.arr0, ENGINES)
        send(root, slot[0], T.sem.arr0)
        return

    rank = T.rank_of(core)
    if rank is None:
        return

    if rank != root_rank:
        g.sync.dma_start(slot[0], T.x[:, :]).then_inc(T.sem.loaded, 16)
        g.wait_ge(T.sem.loaded, 16)
        if rank == 0:
            send(helper, slot[0], T.sem.arr0)
        else:
            send(root, slot[rank], arr[rank])
        return

    def cols(j):
        return T.y[:, j * W:(j + 1) * W]

    g.sync.dma_start(cols(root_rank), T.x[:, :]).then_inc(T.sem.stored_hw, 16)

    g.scalar.wait_ge(T.sem.arr1, ENGINES)
    g.scalar.dma_start(cols(1), slot[1]).then_inc(T.sem.stored_hw, 16)

    g.wait_ge(T.sem.arr3, ENGINES)
    g.dma_start(cols(3), slot[3]).then_inc(T.sem.stored_g, 16)

    g.sync.wait_ge(T.sem.arr0, ENGINES)
    g.sync.dma_start(cols(0), slot[0]).then_inc(T.sem.stored_hw, 16)

    g.wait_ge(T.sem.stored_g, 16)
    g.wait_ge(T.sem.stored_hw, 48)
